import numpy as np, ml_dtypes
CORES = [125,127,253,255,381,383,509,511]
N = 8
import mx_ref
NC, G, S2 = 256, 2, 2
C = np.float32(0.023)
CNT = [[48,40,40,0,96,8,8,16],[40,88,40,16,8,16,48,0],[88,24,32,8,40,16,0,48],[0,8,16,112,0,112,0,8],[48,40,88,8,24,0,16,32],[0,32,8,0,88,0,128,0],[16,0,8,24,0,64,16,128],[16,24,24,88,0,40,40,24]]
OFF = [[sum(c[:e]) for e in range(N + 1)] for c in CNT]
BF = ml_dtypes.bfloat16
def cut(t, i, w=512):
    return t[:, w * i:w * i + w]
def tile(rs):
    return np.stack(rs, axis=2).reshape(128, -1).astype(BF)
def layer(w, X):
    out = []
    for i in range(G):
        for t in range(len(X)):
            p = mx_ref.matmul(mx_ref.quantize(cut(w, len(X) * i + t)), X[t])
            z = p if t == 0 else z + p
        out.append(z)
    return out
def act(Z):
    return [np.maximum(s * z, 0) * C for z in Z for s in (1, -1)]
def setup_inputs(rng):
    def f(*shape):
        return mx_ref.flush((rng.standard_normal(shape, dtype=np.float32) * np.exp2(rng.integers(-2, 3, shape[:-1] + (1,)))).astype(BF))
    gt = (0.125 + 0.875 * rng.random((N, 2, NC))).astype(BF)
    return {"gt": gt, "x": f(N, 128, 4 * NC), "w1": f(N, 128, G * 512), "w2": f(N, 128, 512)}
def setup_inputs_blocks(rng):
    d = setup_inputs(rng)
    for k in ("x", "w1", "w2"): d[k] = mx_ref.spread(d[k], rng, 4)
    return d
def setup_inputs_wide(rng):
    d = setup_inputs(rng)
    for k in ("x", "w1", "w2"): d[k] = mx_ref.flush((d[k].astype(np.float32) * np.exp2(rng.integers(-8, 9, (N, 1, 1))).astype(np.float32)).astype(BF))
    return d
def setup_inputs_zeros(rng):
    d = setup_inputs(rng); v = d["x"].reshape(N, 128, -1, 4).copy()
    v[np.broadcast_to((rng.random((N, 1, v.shape[2], 1)) < 0.33), v.shape)] = 0
    d["x"] = v.reshape(d["x"].shape)
    return d
def reference(gt, x, w1, w2):
    y = np.zeros((N, 128, NC), np.float32); g = gt.astype(np.float32)
    for e in range(N):
        f = (e - S2) % N
        t = np.concatenate([x[j][:, 4 * OFF[j][k]:4 * OFF[j][k + 1]] for k in (e, f) for j in range(N)], axis=1)
        p = mx_ref.matmul(mx_ref.quantize(w2[e]), mx_ref.quantize(tile(act(layer(w1[e], [mx_ref.quantize(t)])))))
        c = 0
        for i, k in enumerate((e, f)):
            for j in range(N):
                a, b = OFF[j][k], OFF[j][k + 1]
                y[j][:, a:b] = y[j][:, a:b] + p[:, c:c + b - a] * g[j, i, a:b]; c += b - a
    return {"y": y}

@@ -1,0 +1,397 @@
+import numpy as np
+from concourse.bass import DstId, RemoteDMATransfer
+from concourse.mybir import dt, AluOpType, ActivationFunctionType
+
+N, NC, S2 = 8, 256, 2
+C = float(np.float32(0.023))
+MIN = 128
+GATE_ROW = 2 * NC
+WIN_MIN = 16
+XPAD = MIN + WIN_MIN
+
+SCRATCH = {
+    "gsrc": ("dram", [128, 4], "bfloat16"), "gls": ("dram", [128, 4], "bfloat16"),
+    "glf0": ("dram", [128, 4], "bfloat16"), "glf1": ("dram", [128, 4], "bfloat16"),
+    "gr": ("sbuf", [128, 4 * GATE_ROW], "bfloat16"), "ga": ("sbuf", [128, 1024], "bfloat16"), "gb": ("sbuf", [128, 1024], "bfloat16"),
+    "wb": ("sbuf", [128, 1536], "bfloat16"),
+    "wq": ("sbuf", [128, 384], "float8_e4m3fn_x4"), "ws": ("sbuf", [128, 384], "uint8"),
+    "vq": ("sbuf", [128, 384], "float8_e4m3fn_x4"), "vs": ("sbuf", [128, 384], "uint8"),
+    "xb": ("sbuf", [128, 4 * (NC + XPAD)], "bfloat16"),
+    "xq": ("sbuf", [128, 1536], "float8_e4m3fn_x4"), "xs": ("sbuf", [128, 1536], "uint8"),
+    "ob": ("sbuf", [128, 1024], "float32"), "tm": ("sbuf", [128, 1024], "float32"),
+    "yb": ("sbuf", [128, 256], "float32"), "ys": ("sbuf", [128, 256], "float32"),
+    "yf0": ("sbuf", [128, 256], "float32"), "yf1": ("sbuf", [128, 256], "float32"),
+}
+SEMAPHORES = ["ld_g", "ld_go", "ld_gl", "ld_w1", "ld_w2", "ld_x", "qw1", "qw2", "qx0", "qx1", "pad", "loc",
+              "a_g", "a_w1", "a_w2", "a_f0", "a_f1", "a_s", "a_yf0", "a_yf1", "a_ys", "gc0", "gc1", "gb0", "gb1",
+              "yv", "yc", "st"]
+for _k in range(4):
+    SCRATCH["h%d" % _k] = ("sbuf", [128, 2048], "bfloat16")
+    SCRATCH["hq%d" % _k] = ("sbuf", [128, 512], "float8_e4m3fn_x4")
+    SCRATCH["hs%d" % _k] = ("sbuf", [128, 512], "uint8")
+    SCRATCH["za%d" % _k] = ("psum", [128, 512], "float32")
+    SCRATCH["zb%d" % _k] = ("psum", [128, 512], "float32")
+    SEMAPHORES += ["%s%d" % (s, _k) for s in ("za", "zb", "as", "av", "q", "p")]
+for _s in ("f0", "f1", "s", "o"):
+    SEMAPHORES += ["eo_" + _s, "ev_" + _s, "t_" + _s]
+
+
+def up(n):
+    return -(-n // WIN_MIN) * WIN_MIN
+
+
+def make_plan(T, topo):
+    cores, cnt = T.cores, T.tables["CNT"]
+    off = [[sum(c[:e]) for e in range(N + 1)] for c in cnt]
+    host = [topo.host(c) for c in cores]
+    P = []
+    for r in range(N):
+        home = [j for j in range(N) if host[j] == host[r]]
+        sib = [j for j in home if j != r][0]
+        place = home.index(r)
+        rack = topo.rack(host[r])
+        far = [j for j in range(N) if topo.rack(host[j]) != rack and topo.may_write(cores[r], cores[j])]
+        other = [j for j in range(N) if topo.rack(host[j]) == rack and host[j] != host[r]]
+        pair = far[place]
+        a, b = (r, pair) if (r + S2) % N == pair else (pair, r)
+        P.append({"sib": sib, "place": place, "pair": pair, "f": other, "a": a, "b": b, "cls": [(a - S2) % N, a, b]})
+    for r in range(N):
+        p = P[r]
+        p["n"] = {j: sum(cnt[j][c] for c in p["cls"]) for j in [r, p["sib"]] + p["f"]}
+        own0 = up(p["n"][p["sib"]])
+        at, win, p["chain"] = own0, {}, {}
+        for q in (r, p["sib"]):
+            c1, c2, c3 = P[q]["cls"]
+            fq = p["f"][P[q]["place"]]
+            d = P[fq]["cls"]
+            assert d[0] == c3 and d[2] == c1
+            runs = []
+            for i, c in enumerate((c1, c2, c3, d[1], c1)):
+                if i == 0:
+                    win[q] = at
+                if i == 2:
+                    win[fq] = at
+                if cnt[r][c]:
+                    if runs and runs[-1][1] + runs[-1][2] == off[r][c]:
+                        runs[-1][2] += cnt[r][c]
+                    else:
+                        runs.append([at, off[r][c], cnt[r][c]])
+                at += cnt[r][c]
+            runs = [[o, s, max(n, MIN)] for o, s, n in runs]
+            at = up(runs[-1][0] + runs[-1][2])
+            runs[-1][2] = at - runs[-1][0]
+            p["chain"][q] = runs
+        p["win"] = win
+        p["land"] = {p["sib"]: own0 - p["n"][p["sib"]], r: own0, p["f"][0]: at, p["f"][1]: at + p["n"][p["f"][0]]}
+        o = 0
+        p["out"] = {}
+        for j in p["f"] + [p["sib"], r]:
+            p["out"][j] = o
+            o += p["n"][j]
+    return P, cnt, off
+
+
+def rank_program(g, core, T, topo):
+    rank = T.rank_of(core)
+    if rank is None:
+        return
+    P, cnt, off = make_plan(T, topo)
+    me = P[rank]
+    cores, sib, F = T.cores, me["sib"], me["f"]
+    add, mult, mx = AluOpType.add, AluOpType.mult, AluOpType.max
+    relu, copy = ActivationFunctionType.Relu, ActivationFunctionType.Copy
+    V, S, Te, Sy = g.vector, g.scalar, g.tensor, g.sync
+    have = {s: 0 for s in SEMAPHORES}
+    seen = {s: 0 for s in SEMAPHORES}
+
+    def inc(ins, name, n=1):
+        ins.then_inc(T.sem[name], n)
+        have[name] += n
+
+    def wait(queue, name):
+        if have[name]:
+            queue.wait_ge(T.sem[name], have[name])
+            seen[name] = have[name]
+
+    def engines(src):
+        m = -1
+        for j in range(N):
+            if j != src and topo.may_write(cores[src], cores[j]):
+                m &= topo.mask(cores[src], cores[j])
+        return [i for i in range(16) if m >> i & 1]
+
+    ALL = engines(rank)
+    EV, OD = ALL[0::2], ALL[1::2]
+    UP = [i for i in range(16) if topo.mask(core, cores[sib]) >> i & 1 and i not in ALL][0:len(OD)]
+
+    def bits(lst):
+        return sum(1 << i for i in lst)
+
+    def send(j, out, in_, eng, sem):
+        rid, pid = topo.addr(cores[j], core)
+        g.remote_dma(out, in_, T.sem[sem], T.sem.loc, pid, rid, bits(eng))
+        have["loc"] += len(eng)
+
+    def codes(t, a, b):
+        return T[t][:, a:b].bitcast(dt.uint8)
+
+    for j in range(N):
+        ej = engines(j)
+        if j in F + [sib] and me["n"][j]:
+            tag = "s" if j == sib else "f%d" % P[j]["place"]
+            have["a_g"] += len(ej[0::2])
+            have["a_" + tag] += 2 * (len(UP) if j == sib else len(ej[1::2]))
+        if j in F + [sib] and P[j]["n"][rank]:
+            have["a_y" + ("s" if j == sib else "f%d" % P[j]["place"])] += len(UP) if j == sib else len(ej)
+        if P[j]["pair"] == rank:
+            have["a_w1"] += 2 * len(ej[0::2])
+            have["a_w2"] += len(ej[0::2])
+
+    inc(Sy.dma_start(T.wb[:, 0:1024], T.w1[:, :]), "ld_w1", 16)
+    inc(S.dma_start(T.gsrc[:], T.gt[:, :]), "ld_g", 16)
+    inc(S.dma_start(T.xb[:, 0:4 * NC], T.x[:, :]), "ld_x", 16)
+    inc(S.dma_start(T.xb[:, 4 * NC:4 * (NC + XPAD)], T.x[:, 0:4 * XPAD]), "ld_x", 16)
+    inc(S.dma_start(T.wb[:, 1024:1536], T.w2[:, :]), "ld_w2", 16)
+    inc(Sy.dma_start(T.gr[0:1, 0:GATE_ROW], T.gt[:, :]), "ld_go", 16)
+
+    to = [j for j in F + [sib] if P[j]["n"][rank]]
+    wait(g, "ld_g")
+    if to:
+        ids, dsts = [], []
+        for j in to:
+            rid, pid = topo.addr(cores[j], core)
+            ids.append(DstId(rid=rid, pnc=pid))
+            dsts.append(T["gls"][:] if j == sib else T["glf%d" % me["place"]][:])
+        g.remote_dma_fused([RemoteDMATransfer(dst_ids=ids, dma_engine_mask=bits(EV), remote_sem=T.sem.a_g, srcs=[T.gsrc[:]], dsts=dsts)],
+                           local_sem=T.sem.loc)
+        have["loc"] += len(EV)
+
+    stages = []
+    for grp in (F, [sib, rank]):
+        for first in (True, False):
+            e = rank if first else me["pair"]
+            lo = 0 if e == me["a"] else 1
+            cl = me["cls"][lo:lo + 2]
+            runs, m = [], 0
+            for j in grp:
+                n = sum(cnt[j][c] for c in cl)
+                if n:
+                    x0 = me["land"][j] + (cnt[j][me["cls"][0]] if lo else 0)
+                    runs.append((j, x0, m, n))
+                    m += n
+            z0 = min([x for _, x, _, _ in runs] or [0])
+            z1 = max([x + n for _, x, _, n in runs] or [0])
+            if z1 - z0 < MIN:
+                if grp is F:
+                    z0 = z1 - MIN
+                else:
+                    z1 = z0 + MIN
+            assert z1 - z0 <= 512
+            stages.append({"grp": grp, "lo": lo, "cl": cl, "runs": runs, "m": m, "mp": max(m, MIN), "z0": z0, "z1": z1, "own": first})
+    stages = [stages[0], stages[2], stages[1], stages[3]]
+    at = 0
+    for st in stages:
+        st["g0"] = at
+        at += st["m"]
+    gcut = stages[2]["g0"]
+    gend = at
+
+    for k, st in enumerate(stages):
+        if st["m"] and st["m"] < MIN:
+            inc(V.memset(T["h%d" % k][:, 4 * st["m"]:4 * MIN], 0.0), "pad")
+
+    wait(V, "ld_w1")
+    inc(V.quantize_mx(T.wq[:, 0:256], T.ws[:, 0:256], T.wb[:, 0:1024]), "qw1")
+    wait(V, "ld_x")
+    big = max(F, key=lambda j: P[j]["n"][rank])
+    chains = sorted((rank, sib), key=lambda q: P[q]["place"] != P[big]["place"])
+    for i, q in enumerate(chains):
+        end = 0
+        for o, s, n in me["chain"][q]:
+            if o < end:
+                wait(V, "qx%d" % i)
+            end = o + n
+            inc(V.quantize_mx(T.xq[:, o:o + n], T.xs[:, o:o + n], T.xb[:, 4 * s:4 * (s + n)]), "qx%d" % i)
+    wait(V, "ld_w2")
+    inc(V.quantize_mx(T.wq[:, 256:384], T.ws[:, 256:384], T.wb[:, 1024:1536]), "qw2")
+
+    def send_x(j):
+        n = P[j]["n"][rank]
+        if n:
+            a, b, tag = me["win"][j], P[j]["land"][rank], "a_s" if j == sib else "a_f%d" % me["place"]
+            eng = UP if j == sib else OD
+            send(j, codes("xq", b, b + n), codes("xq", a, a + n), eng, tag)
+            send(j, T.xs[:, b:b + n], T.xs[:, a:a + n], eng, tag)
+
+    wait(g, "qw1")
+    send(me["pair"], codes("vq", 0, 256), codes("wq", 0, 256), EV, "a_w1")
+    for i, q in enumerate(chains):
+        wait(g, "qx%d" % i)
+        send_x(F[P[q]["place"]])
+    wait(g, "qw2")
+    send(me["pair"], T.vs[:, 0:384], T.ws[:, 0:384], EV, "a_w1")
+    send(me["pair"], codes("vq", 256, 384), codes("wq", 256, 384), EV, "a_w2")
+    send_x(sib)
+
+    wait(Sy, "a_g")
+    rows = {rank: 0}
+    for i, j in enumerate([j for j in F + [sib] if me["n"][j]]):
+        rows[j] = (i + 1) * GATE_ROW
+        src = T.gls if j == sib else T["glf%d" % P[j]["place"]]
+        inc(Sy.dma_start(T.gr[0:1, rows[j]:rows[j] + GATE_ROW], src[:]), "ld_gl", 16)
+    wait(S, "ld_go")
+    wait(S, "ld_gl")
+    for half in (0, 1):
+        for st in stages[2 * half:2 * half + 2]:
+            for j, x0, m, n in st["runs"]:
+                d = st["g0"] + m
+                for c, row in ((st["cl"][0], 1), (st["cl"][1], 0)):
+                    if cnt[j][c]:
+                        s = rows[j] + row * NC + off[j][c]
+                        inc(S.activation(T.ga[0:1, d:d + cnt[j][c]], T.gr[0:1, s:s + cnt[j][c]], copy), "gc%d" % half)
+                        d += cnt[j][c]
+        a, b = (0, gcut) if half == 0 else (gcut, gend)
+        wait(g, "gc%d" % half)
+        if b > a:
+            inc(g.partition_broadcast(T.gb[:, a:b], T.ga[0:1, a:b], 128), "gb%d" % half)
+
+    def front(k):
+        st = stages[k]
+        if not st["m"]:
+            return
+        q, s = ("wq", "ws") if st["own"] else ("vq", "vs")
+        for i, z in enumerate(("za%d" % k, "zb%d" % k)):
+            inc(Te.matmul_mx(T[z][:, 0:st["z1"] - st["z0"]], T[q][:, 128 * i:128 * i + 128], T[s][:, 128 * i:128 * i + 128],
+                             T.xq[:, st["z0"]:st["z1"]], T.xs[:, st["z0"]:st["z1"]], True, True), z)
+
+    def middle(k):
+        st = stages[k]
+        if not st["m"]:
+            return
+        h = T["h%d" % k]
+        wait(S, "za%d" % k)
+        wait(V, "zb%d" % k)
+        for j, x0, m, n in st["runs"]:
+            c = x0 - st["z0"]
+            for i, sgn in enumerate((C, -C)):
+                inc(S.activation(h[:, 4 * m + i:4 * (m + n):4], T["za%d" % k][:, c:c + n], relu, scale=sgn), "as%d" % k)
+                inc(V.tensor_scalar(h[:, 4 * m + 2 + i:4 * (m + n):4], T["zb%d" % k][:, c:c + n], sgn, 0.0, mult, mx), "av%d" % k)
+        wait(V, "pad")
+        wait(V, "as%d" % k)
+        wait(V, "av%d" % k)
+        inc(V.quantize_mx(T["hq%d" % k][:, 0:st["mp"]], T["hs%d" % k][:, 0:st["mp"]], h[:, 0:4 * st["mp"]]), "q%d" % k)
+
+    def back(k):
+        st = stages[k]
+        if not st["m"]:
+            return
+        q, s = ("wq", "ws") if st["own"] else ("vq", "vs")
+        wait(Te, "q%d" % k)
+        inc(Te.matmul_mx(T["za%d" % k][:, 0:st["mp"]], T[q][:, 256:384], T[s][:, 256:384],
+                         T["hq%d" % k][:, 0:st["mp"]], T["hs%d" % k][:, 0:st["mp"]], True, True), "p%d" % k)
+
+    def tag_of(j):
+        return "o" if j == rank else "s" if j == sib else "f%d" % P[j]["place"]
+
+    def evac(k, j):
+        st = stages[k]
+        for jj, x0, m, n in st["runs"]:
+            if jj != j:
+                continue
+            za, tag = T["za%d" % k], tag_of(j)
+            ng = [cnt[j][c] for c in me["cls"]]
+            o = me["out"][j]
+            o2 = o + ng[0]
+            g0 = st["g0"] + m
+            if st["own"]:
+                b = o + (ng[0] if st["lo"] else 0)
+                inc(V.tensor_tensor(T.ob[:, b:b + n], za[:, m:m + n], T.gb[:, g0:g0 + n], mult), "eo_" + tag)
+                continue
+            n2, nx = ng[1], n - ng[1]
+            m2, m1, bx = (m, m + n2, o2 + n2) if st["lo"] else (m + nx, m, o)
+            if n2:
+                inc(V.tensor_tensor(T.tm[:, o2:o2 + n2], za[:, m2:m2 + n2], T.gb[:, g0 + m2 - m:g0 + m2 - m + n2], mult), "t_" + tag)
+            if nx:
+                inc(V.tensor_tensor(T.ob[:, bx:bx + nx], za[:, m1:m1 + nx], T.gb[:, g0 + m1 - m:g0 + m1 - m + nx], mult), "ev_" + tag)
+            if n2:
+                wait(V, "t_" + tag)
+                wait(V, "eo_" + tag)
+                y0 = off[rank][me["cls"][1]]
+                out = T.yb[:, y0:y0 + n2] if j == rank else T.ob[:, o2:o2 + n2]
+                inc(V.tensor_tensor(out, T.ob[:, o2:o2 + n2], T.tm[:, o2:o2 + n2], add), "yv" if j == rank else "ev_" + tag)
+
+    wait(Te, "qw1")
+    wait(Te, "qx0")
+    wait(Te, "qx1")
+    wait(Te, "a_f0")
+    wait(Te, "a_f1")
+    front(0)
+    wait(Te, "a_s")
+    front(1)
+    middle(0)
+    middle(1)
+    wait(Te, "qw2")
+    back(0)
+    back(1)
+
+    wait(Te, "a_w1")
+    front(2)
+    front(3)
+    middle(2)
+    middle(3)
+    wait(Te, "a_w2")
+    back(2)
+    back(3)
+    for k in (0, 1):
+        if stages[k]["m"]:
+            wait(V, "p%d" % k)
+            wait(V, "gb0")
+        for j in stages[k]["grp"]:
+            evac(k, j)
+    for k in (2, 3):
+        if stages[k]["m"]:
+            wait(V, "p%d" % k)
+            wait(V, "gb1")
+        for j in stages[k]["grp"]:
+            evac(k, j)
+            n = me["n"][j]
+            if j != rank and n:
+                wait(g, "eo_" + tag_of(j))
+                wait(g, "ev_" + tag_of(j))
+                land = "ys" if j == sib else "yf%d" % me["place"]
+                send(j, T[land][:, 0:n], T.ob[:, me["out"][j]:me["out"][j] + n], UP if j == sib else ALL, "a_" + land)
+
+    for q in (rank, sib):
+        R = F[P[q]["place"]]
+        yf = "yf%d" % P[q]["place"]
+        c1, c2, c3 = P[q]["cls"]
+        d1, d2, d3 = P[R]["cls"]
+        ln, rn = [cnt[rank][c] for c in (c1, c2, c3)], [cnt[rank][c] for c in (d1, d2, d3)]
+        wait(S, "a_" + yf)
+        if rn[1]:
+            y0 = off[rank][d2]
+            inc(S.activation(T.yb[:, y0:y0 + rn[1]], T[yf][:, rn[0]:rn[0] + rn[1]], copy), "yc")
+        if q == rank:
+            wait(V, "eo_o")
+            wait(V, "ev_o")
+            loc, lb = T.ob, me["out"][rank]
+        else:
+            wait(V, "a_ys")
+            wait(S, "a_ys")
+            if ln[1]:
+                y0 = off[rank][c2]
+                inc(S.activation(T.yb[:, y0:y0 + ln[1]], T.ys[:, ln[0]:ln[0] + ln[1]], copy), "yc")
+            loc, lb = T.ys, 0
+        wait(V, "a_" + yf)
+        for c, l, r in ((c1, lb, rn[0] + rn[1]), (c3, lb + ln[0] + ln[1], 0)):
+            n = cnt[rank][c]
+            if n:
+                y0 = off[rank][c]
+                inc(V.tensor_tensor(T.yb[:, y0:y0 + n], loc[:, l:l + n], T[yf][:, r:r + n], add), "yv")
+    wait(Sy, "yv")
+    wait(Sy, "yc")
+    inc(Sy.dma_start(T.y[:, :], T.yb[:]), "st", 16)
+    wait(Sy, "st")
+    wait(g, "loc")
+    for q in SEMAPHORES:
+        assert seen[q] == have[q], q

@@ -3,40 +3,78 @@ from concourse.bass import DstId, RemoteDMATransfer
 from concourse.mybir import dt, AluOpType, ActivationFunctionType
 
 N, NC, S2 = 8, 256, 2
+WORLD = 512
 C = float(np.float32(0.023))
 MIN = 128
 GATE_ROW = 2 * NC
 WIN_MIN = 16
-XPAD = MIN + WIN_MIN
 
 SCRATCH = {
     "gsrc": ("dram", [128, 4], "bfloat16"), "gls": ("dram", [128, 4], "bfloat16"),
     "glf0": ("dram", [128, 4], "bfloat16"), "glf1": ("dram", [128, 4], "bfloat16"),
     "gr": ("sbuf", [128, 4 * GATE_ROW], "bfloat16"), "ga": ("sbuf", [128, 1024], "bfloat16"), "gb": ("sbuf", [128, 1024], "bfloat16"),
-    "wb": ("sbuf", [128, 1536], "bfloat16"),
+    "wb": ("sbuf", [128, 1024], "bfloat16"),
     "wq": ("sbuf", [128, 384], "float8_e4m3fn_x4"), "ws": ("sbuf", [128, 384], "uint8"),
     "vq": ("sbuf", [128, 384], "float8_e4m3fn_x4"), "vs": ("sbuf", [128, 384], "uint8"),
-    "xb": ("sbuf", [128, 4 * (NC + XPAD)], "bfloat16"),
+    "xb": ("sbuf", [128, 4 * (NC + MIN)], "bfloat16"),
     "xq": ("sbuf", [128, 1536], "float8_e4m3fn_x4"), "xs": ("sbuf", [128, 1536], "uint8"),
     "ob": ("sbuf", [128, 1024], "float32"), "tm": ("sbuf", [128, 1024], "float32"),
     "yb": ("sbuf", [128, 256], "float32"), "ys": ("sbuf", [128, 256], "float32"),
     "yf0": ("sbuf", [128, 256], "float32"), "yf1": ("sbuf", [128, 256], "float32"),
 }
-SEMAPHORES = ["ld_g", "ld_go", "ld_gl", "ld_w1", "ld_w2", "ld_x", "qw1", "qw2", "qx0", "qx1", "pad", "loc",
-              "a_g", "a_w1", "a_w2", "a_f0", "a_f1", "a_s", "a_yf0", "a_yf1", "a_ys", "gc0", "gc1", "gb0", "gb1",
-              "yv", "yc", "st"]
-for _k in range(4):
+SEMAPHORES = ["ld_g", "ld_go", "ld_gl", "ld_w1", "ld_w2", "ld_x", "qw1", "qw2", "qx0", "qx1", "pad", "loc", "o_w1", "o_w2", "o_ws",
+              "a_g", "a_w1", "a_w2", "a_ws", "a_f0", "a_f1", "a_s", "a_yf0", "a_yf1", "a_ye0", "a_ye1", "a_ys", "yv", "yc", "st"]
+for _k in range(2):
     SCRATCH["h%d" % _k] = ("sbuf", [128, 2048], "bfloat16")
     SCRATCH["hq%d" % _k] = ("sbuf", [128, 512], "float8_e4m3fn_x4")
     SCRATCH["hs%d" % _k] = ("sbuf", [128, 512], "uint8")
     SCRATCH["za%d" % _k] = ("psum", [128, 512], "float32")
     SCRATCH["zb%d" % _k] = ("psum", [128, 512], "float32")
-    SEMAPHORES += ["%s%d" % (s, _k) for s in ("za", "zb", "as", "av", "q", "p")]
+    SEMAPHORES += ["%s%d" % (s, _k) for s in ("za", "zb", "as", "av", "q", "p", "gc", "gb")]
 for _s in ("f0", "f1", "s", "o"):
     SEMAPHORES += ["eo_" + _s, "ev_" + _s, "t_" + _s]
+_HELP = {}
 
 
-def up(n):
+def helper(c, topo):
+    if c not in _HELP:
+        def port(k):
+            return any(topo.mates(k, d) and topo.may_write(k, d) for d in range(WORLD))
+        _HELP[c] = [k for k in range(WORLD) if topo.host(k) == topo.host(c) and topo.chip(k) == topo.chip(c)
+                    and topo.die(k) != topo.die(c) and port(k) == port(c)][0]
+    return _HELP[c]
+
+
+def bits(lst):
+    return sum(1 << i for i in lst)
+
+
+def listed(mask):
+    return [i for i in range(16) if mask >> i & 1]
+
+
+def far_engines(cores, src, topo):
+    m = -1
+    for d in cores:
+        if d != src and topo.may_write(src, d):
+            m &= topo.mask(src, d)
+    return listed(m)
+
+
+def near_engines(cores, src, dst, topo):
+    off = far_engines(cores, src, topo)
+    return [i for i in listed(topo.mask(src, dst)) if i not in off]
+
+
+def w1_engines(far):
+    return far[0::2]
+
+
+def token_engines(far, i):
+    return far[1::2] if i == 0 else far[0::2]
+
+
+def up16(n):
     return -(-n // WIN_MIN) * WIN_MIN
 
 
@@ -54,11 +92,12 @@ def make_plan(T, topo):
         other = [j for j in range(N) if topo.rack(host[j]) == rack and host[j] != host[r]]
         pair = far[place]
         a, b = (r, pair) if (r + S2) % N == pair else (pair, r)
-        P.append({"sib": sib, "place": place, "pair": pair, "f": other, "a": a, "b": b, "cls": [(a - S2) % N, a, b]})
+        P.append({"sib": sib, "place": place, "pair": pair, "f": other, "a": a, "b": b, "cls": [(a - S2) % N, a, b],
+                  "early": 0 if r == a else 2})
     for r in range(N):
         p = P[r]
         p["n"] = {j: sum(cnt[j][c] for c in p["cls"]) for j in [r, p["sib"]] + p["f"]}
-        own0 = up(p["n"][p["sib"]])
+        own0 = up16(p["n"][p["sib"]])
         at, win, p["chain"] = own0, {}, {}
         for q in (r, p["sib"]):
             c1, c2, c3 = P[q]["cls"]
@@ -78,26 +117,44 @@ def make_plan(T, topo):
                         runs.append([at, off[r][c], cnt[r][c]])
                 at += cnt[r][c]
             runs = [[o, s, max(n, MIN)] for o, s, n in runs]
-            at = up(runs[-1][0] + runs[-1][2])
+            at = up16(runs[-1][0] + runs[-1][2])
             runs[-1][2] = at - runs[-1][0]
             p["chain"][q] = runs
-        p["win"] = win
-        p["land"] = {p["sib"]: own0 - p["n"][p["sib"]], r: own0, p["f"][0]: at, p["f"][1]: at + p["n"][p["f"][0]]}
-        o = 0
+            assert max(s + n for o, s, n in runs) <= NC + MIN
+        p["win"], p["end"] = win, at
+        p["land"] = {p["sib"]: own0 - p["n"][p["sib"]], r: own0,
+                     p["f"][0]: 0, p["f"][1]: p["n"][p["f"][0]]}
         p["out"] = {}
-        for j in p["f"] + [p["sib"], r]:
-            p["out"][j] = o
-            o += p["n"][j]
+        for grp in (p["f"], [p["sib"], r]):
+            o = 0
+            for j in grp:
+                p["out"][j] = o
+                o += p["n"][j]
+    for r in range(N):
+        p = P[r]
+        p["sent"] = dict(p["n"])
+        j = p["f"][1]
+        if p["n"][j]:
+            p["sent"][j] = max(p["n"][j], MIN - p["n"][p["f"][0]])
+        assert sum(p["sent"][j] for j in p["f"]) >= MIN and P[j]["win"][r] + p["sent"][j] <= P[j]["end"]
+        big = max(p["f"], key=lambda j: P[j]["n"][r])
+        p["order"] = sorted((r, p["sib"]), key=lambda q: P[q]["place"] != P[big]["place"])
     return P, cnt, off
 
 
 def rank_program(g, core, T, topo):
+    cores = T.cores
     rank = T.rank_of(core)
-    if rank is None:
-        return
+    is_rank = rank is not None
+    if not is_rank:
+        mine = [r for r in range(N) if helper(cores[r], topo) == core]
+        if not mine:
+            return
+        rank = mine[0]
     P, cnt, off = make_plan(T, topo)
     me = P[rank]
-    cores, sib, F = T.cores, me["sib"], me["f"]
+    R, H = cores[rank], helper(cores[rank], topo)
+    sib, F, pair = me["sib"], me["f"], me["pair"]
     add, mult, mx = AluOpType.add, AluOpType.mult, AluOpType.max
     relu, copy = ActivationFunctionType.Relu, ActivationFunctionType.Copy
     V, S, Te, Sy = g.vector, g.scalar, g.tensor, g.sync
@@ -113,147 +170,160 @@ def rank_program(g, core, T, topo):
             queue.wait_ge(T.sem[name], have[name])
             seen[name] = have[name]
 
-    def engines(src):
-        m = -1
-        for j in range(N):
-            if j != src and topo.may_write(cores[src], cores[j]):
-                m &= topo.mask(cores[src], cores[j])
-        return [i for i in range(16) if m >> i & 1]
+    def far(src):
+        return far_engines(cores, src, topo)
 
-    ALL = engines(rank)
-    EV, OD = ALL[0::2], ALL[1::2]
-    UP = [i for i in range(16) if topo.mask(core, cores[sib]) >> i & 1 and i not in ALL][0:len(OD)]
+    def near(src, dst):
+        return near_engines(cores, src, dst, topo)
 
-    def bits(lst):
-        return sum(1 << i for i in lst)
+    def help_of(j):
+        return helper(cores[j], topo)
 
-    def send(j, out, in_, eng, sem):
-        rid, pid = topo.addr(cores[j], core)
+    def send(d, out, in_, eng, sem):
+        rid, pid = topo.addr(d, core)
         g.remote_dma(out, in_, T.sem[sem], T.sem.loc, pid, rid, bits(eng))
         have["loc"] += len(eng)
 
     def codes(t, a, b):
         return T[t][:, a:b].bitcast(dt.uint8)
 
-    for j in range(N):
-        ej = engines(j)
-        if j in F + [sib] and me["n"][j]:
-            tag = "s" if j == sib else "f%d" % P[j]["place"]
-            have["a_g"] += len(ej[0::2])
-            have["a_" + tag] += 2 * (len(UP) if j == sib else len(ej[1::2]))
-        if j in F + [sib] and P[j]["n"][rank]:
-            have["a_y" + ("s" if j == sib else "f%d" % P[j]["place"])] += len(UP) if j == sib else len(ej)
-        if P[j]["pair"] == rank:
-            have["a_w1"] += 2 * len(ej[0::2])
-            have["a_w2"] += len(ej[0::2])
+    def early_n(r, j):
+        return cnt[j][P[r]["cls"][P[r]["early"]]]
 
-    inc(Sy.dma_start(T.wb[:, 0:1024], T.w1[:, :]), "ld_w1", 16)
-    inc(S.dma_start(T.gsrc[:], T.gt[:, :]), "ld_g", 16)
-    inc(S.dma_start(T.xb[:, 0:4 * NC], T.x[:, :]), "ld_x", 16)
-    inc(S.dma_start(T.xb[:, 4 * NC:4 * (NC + XPAD)], T.x[:, 0:4 * XPAD]), "ld_x", 16)
-    inc(S.dma_start(T.wb[:, 1024:1536], T.w2[:, :]), "ld_w2", 16)
-    inc(Sy.dma_start(T.gr[0:1, 0:GATE_ROW], T.gt[:, :]), "ld_go", 16)
+    if is_rank:
+        sources = [sib]
+        if me["n"][sib]:
+            have["a_g"] += len(far(cores[sib])[0::2])
+            have["a_s"] += 2 * len(near(cores[sib], core))
+        if P[sib]["n"][rank]:
+            have["a_ys"] += len(near(cores[sib], core))
+        for s in ("a_w1", "a_ws", "a_w2"):
+            have[s] += len(near(H, core))
+        for j in F:
+            ne = early_n(j, rank)
+            if ne:
+                have["a_ye%d" % P[j]["place"]] += len(far(help_of(j)))
+            if P[j]["n"][rank] > ne:
+                have["a_yf%d" % P[j]["place"]] += len(far(help_of(j)))
+    else:
+        sources = F
+        for j in F:
+            if me["n"][j]:
+                have["a_g"] += len(far(cores[j])[0::2])
+                i = [P[q]["place"] for q in P[j]["order"]].index(me["place"])
+                have["a_f%d" % P[j]["place"]] += 2 * len(token_engines(far(cores[j]), i))
+        for s in ("o_w1", "o_w2", "o_ws"):
+            have[s] += len(near(R, core))
+        have["a_w1"] += len(w1_engines(far(cores[pair])))
+        for s in ("a_w2", "a_ws"):
+            have[s] += len(far(help_of(pair)))
 
-    to = [j for j in F + [sib] if P[j]["n"][rank]]
-    wait(g, "ld_g")
-    if to:
-        ids, dsts = [], []
-        for j in to:
-            rid, pid = topo.addr(cores[j], core)
-            ids.append(DstId(rid=rid, pnc=pid))
-            dsts.append(T["gls"][:] if j == sib else T["glf%d" % me["place"]][:])
-        g.remote_dma_fused([RemoteDMATransfer(dst_ids=ids, dma_engine_mask=bits(EV), remote_sem=T.sem.a_g, srcs=[T.gsrc[:]], dsts=dsts)],
-                           local_sem=T.sem.loc)
-        have["loc"] += len(EV)
+    grp = [sib, rank] if is_rank else F
+    stages, at = [], 0
+    for first in (True, False):
+        e = rank if first else pair
+        lo = 0 if e == me["a"] else 1
+        cl = me["cls"][lo:lo + 2]
+        runs, m = [], 0
+        for j in grp:
+            n = sum(cnt[j][c] for c in cl)
+            if n:
+                x0 = me["land"][j] + (cnt[j][me["cls"][0]] if lo else 0)
+                runs.append((j, x0, m, n))
+                m += n
+        z0 = min([x for _, x, _, _ in runs] or [0])
+        z1 = max([x + n for _, x, _, n in runs] or [0])
+        if z1 - z0 < MIN:
+            if not is_rank:
+                z0 = max(0, z1 - MIN)
+            z1 = z0 + MIN
+        assert z1 - z0 <= 512
+        stages.append({"lo": lo, "cl": cl, "runs": runs, "m": m, "mp": max(m, MIN), "z0": z0, "z1": z1, "own": first, "g0": at})
+        at += m
 
-    stages = []
-    for grp in (F, [sib, rank]):
-        for first in (True, False):
-            e = rank if first else me["pair"]
-            lo = 0 if e == me["a"] else 1
-            cl = me["cls"][lo:lo + 2]
-            runs, m = [], 0
-            for j in grp:
-                n = sum(cnt[j][c] for c in cl)
-                if n:
-                    x0 = me["land"][j] + (cnt[j][me["cls"][0]] if lo else 0)
-                    runs.append((j, x0, m, n))
-                    m += n
-            z0 = min([x for _, x, _, _ in runs] or [0])
-            z1 = max([x + n for _, x, _, n in runs] or [0])
-            if z1 - z0 < MIN:
-                if grp is F:
-                    z0 = z1 - MIN
-                else:
-                    z1 = z0 + MIN
-            assert z1 - z0 <= 512
-            stages.append({"grp": grp, "lo": lo, "cl": cl, "runs": runs, "m": m, "mp": max(m, MIN), "z0": z0, "z1": z1, "own": first})
-    stages = [stages[0], stages[2], stages[1], stages[3]]
-    at = 0
-    for st in stages:
-        st["g0"] = at
-        at += st["m"]
-    gcut = stages[2]["g0"]
-    gend = at
+    if is_rank:
+        NEAR, NSIB = near(core, H), near(core, cores[sib])
+        EV = far(core)[0::2]
+        inc(Sy.dma_start(T.xb[:, 4 * NC:4 * (NC + MIN)], T.w2[:, :]), "ld_w2", 16)
+        inc(S.dma_start(T.gsrc[:], T.gt[:, :]), "ld_g", 16)
+        inc(S.dma_start(T.wb[:, 0:1024], T.w1[:, :]), "ld_w1", 16)
+        inc(Sy.dma_start(T.xb[:, 0:4 * NC], T.x[:, :]), "ld_x", 16)
+        inc(Sy.dma_start(T.gr[0:1, 0:GATE_ROW], T.gt[:, :]), "ld_go", 16)
+
+        to = [j for j in F + [sib] if P[j]["n"][rank]]
+        wait(g, "ld_g")
+        if to:
+            ids, dsts = [], []
+            for j in to:
+                rid, pid = topo.addr(cores[j] if j == sib else help_of(j), core)
+                ids.append(DstId(rid=rid, pnc=pid))
+                dsts.append(T["gls"][:] if j == sib else T["glf%d" % me["place"]][:])
+            g.remote_dma_fused([RemoteDMATransfer(dst_ids=ids, dma_engine_mask=bits(EV), remote_sem=T.sem.a_g, srcs=[T.gsrc[:]], dsts=dsts)],
+                               local_sem=T.sem.loc)
+            have["loc"] += len(EV)
 
     for k, st in enumerate(stages):
         if st["m"] and st["m"] < MIN:
             inc(V.memset(T["h%d" % k][:, 4 * st["m"]:4 * MIN], 0.0), "pad")
 
-    wait(V, "ld_w1")
-    inc(V.quantize_mx(T.wq[:, 0:256], T.ws[:, 0:256], T.wb[:, 0:1024]), "qw1")
-    wait(V, "ld_x")
-    big = max(F, key=lambda j: P[j]["n"][rank])
-    chains = sorted((rank, sib), key=lambda q: P[q]["place"] != P[big]["place"])
-    for i, q in enumerate(chains):
-        end = 0
-        for o, s, n in me["chain"][q]:
-            if o < end:
-                wait(V, "qx%d" % i)
-            end = o + n
-            inc(V.quantize_mx(T.xq[:, o:o + n], T.xs[:, o:o + n], T.xb[:, 4 * s:4 * (s + n)]), "qx%d" % i)
-    wait(V, "ld_w2")
-    inc(V.quantize_mx(T.wq[:, 256:384], T.ws[:, 256:384], T.wb[:, 1024:1536]), "qw2")
+    if is_rank:
+        wait(V, "ld_w2")
+        inc(V.quantize_mx(T.wq[:, 256:384], T.ws[:, 256:384], T.xb[:, 4 * NC:4 * (NC + MIN)]), "qw2")
+        wait(V, "ld_w1")
+        inc(V.quantize_mx(T.wq[:, 0:256], T.ws[:, 0:256], T.wb[:, 0:1024]), "qw1")
+        wait(V, "ld_x")
+        for i, q in enumerate(me["order"]):
+            end = 0
+            for o, s, n in me["chain"][q]:
+                if o < end:
+                    wait(V, "qx%d" % i)
+                end = o + n
+                inc(V.quantize_mx(T.xq[:, o:o + n], T.xs[:, o:o + n], T.xb[:, 4 * s:4 * (s + n)]), "qx%d" % i)
 
-    def send_x(j):
-        n = P[j]["n"][rank]
-        if n:
-            a, b, tag = me["win"][j], P[j]["land"][rank], "a_s" if j == sib else "a_f%d" % me["place"]
-            eng = UP if j == sib else OD
-            send(j, codes("xq", b, b + n), codes("xq", a, a + n), eng, tag)
-            send(j, T.xs[:, b:b + n], T.xs[:, a:a + n], eng, tag)
+        def send_x(j, d, tag, eng):
+            if P[j]["n"][rank]:
+                n, a, b = P[j]["sent"][rank], me["win"][j], P[j]["land"][rank]
+                send(d, codes("xq", b, b + n), codes("xq", a, a + n), eng, tag)
+                send(d, T.xs[:, b:b + n], T.xs[:, a:a + n], eng, tag)
 
-    wait(g, "qw1")
-    send(me["pair"], codes("vq", 0, 256), codes("wq", 0, 256), EV, "a_w1")
-    for i, q in enumerate(chains):
-        wait(g, "qx%d" % i)
-        send_x(F[P[q]["place"]])
-    wait(g, "qw2")
-    send(me["pair"], T.vs[:, 0:384], T.ws[:, 0:384], EV, "a_w1")
-    send(me["pair"], codes("vq", 256, 384), codes("wq", 256, 384), EV, "a_w2")
-    send_x(sib)
+        wait(g, "qw2")
+        send(H, codes("wq", 256, 384), codes("wq", 256, 384), NEAR, "o_w2")
+        wait(g, "qw1")
+        send(help_of(pair), codes("vq", 0, 256), codes("wq", 0, 256), w1_engines(far(core)), "a_w1")
+        send(H, T.ws[:, 0:384], T.ws[:, 0:384], NEAR, "o_ws")
+        for i, q in enumerate(me["order"]):
+            wait(g, "qx%d" % i)
+            j = F[P[q]["place"]]
+            send_x(j, help_of(j), "a_f%d" % me["place"], token_engines(far(core), i))
+            if i == 0:
+                send(H, codes("wq", 0, 256), codes("wq", 0, 256), NEAR, "o_w1")
+        send_x(sib, cores[sib], "a_s", NSIB)
+    else:
+        ALL, NEAR = far(core), near(core, R)
+        wait(g, "o_w2")
+        send(help_of(pair), codes("vq", 256, 384), codes("wq", 256, 384), ALL, "a_w2")
+        wait(g, "o_ws")
+        send(help_of(pair), T.vs[:, 0:384], T.ws[:, 0:384], ALL, "a_ws")
 
     wait(Sy, "a_g")
     rows = {rank: 0}
-    for i, j in enumerate([j for j in F + [sib] if me["n"][j]]):
+    for i, j in enumerate([j for j in sources if me["n"][j]]):
         rows[j] = (i + 1) * GATE_ROW
         src = T.gls if j == sib else T["glf%d" % P[j]["place"]]
         inc(Sy.dma_start(T.gr[0:1, rows[j]:rows[j] + GATE_ROW], src[:]), "ld_gl", 16)
     wait(S, "ld_go")
     wait(S, "ld_gl")
-    for half in (0, 1):
-        for st in stages[2 * half:2 * half + 2]:
-            for j, x0, m, n in st["runs"]:
-                d = st["g0"] + m
-                for c, row in ((st["cl"][0], 1), (st["cl"][1], 0)):
-                    if cnt[j][c]:
-                        s = rows[j] + row * NC + off[j][c]
-                        inc(S.activation(T.ga[0:1, d:d + cnt[j][c]], T.gr[0:1, s:s + cnt[j][c]], copy), "gc%d" % half)
-                        d += cnt[j][c]
-        a, b = (0, gcut) if half == 0 else (gcut, gend)
-        wait(g, "gc%d" % half)
-        if b > a:
-            inc(g.partition_broadcast(T.gb[:, a:b], T.ga[0:1, a:b], 128), "gb%d" % half)
+    for k, st in enumerate(stages):
+        for j, x0, m, n in st["runs"]:
+            d = st["g0"] + m
+            for c, row in ((st["cl"][0], 1), (st["cl"][1], 0)):
+                if cnt[j][c]:
+                    s = rows[j] + row * NC + off[j][c]
+                    inc(S.activation(T.ga[0:1, d:d + cnt[j][c]], T.gr[0:1, s:s + cnt[j][c]], copy), "gc%d" % k)
+                    d += cnt[j][c]
+        if st["m"]:
+            wait(g, "gc%d" % k)
+            inc(g.partition_broadcast(T.gb[:, st["g0"]:st["g0"] + st["m"]], T.ga[0:1, st["g0"]:st["g0"] + st["m"]], 128), "gb%d" % k)
 
     def front(k):
         st = stages[k]
@@ -320,78 +390,90 @@ def rank_program(g, core, T, topo):
                 out = T.yb[:, y0:y0 + n2] if j == rank else T.ob[:, o2:o2 + n2]
                 inc(V.tensor_tensor(out, T.ob[:, o2:o2 + n2], T.tm[:, o2:o2 + n2], add), "yv" if j == rank else "ev_" + tag)
 
-    wait(Te, "qw1")
-    wait(Te, "qx0")
-    wait(Te, "qx1")
-    wait(Te, "a_f0")
-    wait(Te, "a_f1")
+    for s in ("qw1", "qw2", "qx0", "qx1", "a_s") if is_rank else ("o_w1", "o_ws", "a_f0", "a_f1"):
+        wait(Te, s)
     front(0)
-    wait(Te, "a_s")
-    front(1)
     middle(0)
-    middle(1)
-    wait(Te, "qw2")
+    wait(Te, "o_w2")
     back(0)
-    back(1)
+    if stages[0]["m"]:
+        wait(V, "p0")
+        wait(V, "gb0")
+    for j in grp:
+        evac(0, j)
 
     wait(Te, "a_w1")
-    front(2)
-    front(3)
-    middle(2)
-    middle(3)
-    wait(Te, "a_w2")
-    back(2)
-    back(3)
-    for k in (0, 1):
-        if stages[k]["m"]:
-            wait(V, "p%d" % k)
-            wait(V, "gb0")
-        for j in stages[k]["grp"]:
-            evac(k, j)
-    for k in (2, 3):
-        if stages[k]["m"]:
-            wait(V, "p%d" % k)
-            wait(V, "gb1")
-        for j in stages[k]["grp"]:
-            evac(k, j)
-            n = me["n"][j]
-            if j != rank and n:
-                wait(g, "eo_" + tag_of(j))
-                wait(g, "ev_" + tag_of(j))
-                land = "ys" if j == sib else "yf%d" % me["place"]
-                send(j, T[land][:, 0:n], T.ob[:, me["out"][j]:me["out"][j] + n], UP if j == sib else ALL, "a_" + land)
-
-    for q in (rank, sib):
-        R = F[P[q]["place"]]
-        yf = "yf%d" % P[q]["place"]
-        c1, c2, c3 = P[q]["cls"]
-        d1, d2, d3 = P[R]["cls"]
-        ln, rn = [cnt[rank][c] for c in (c1, c2, c3)], [cnt[rank][c] for c in (d1, d2, d3)]
-        wait(S, "a_" + yf)
-        if rn[1]:
-            y0 = off[rank][d2]
-            inc(S.activation(T.yb[:, y0:y0 + rn[1]], T[yf][:, rn[0]:rn[0] + rn[1]], copy), "yc")
-        if q == rank:
-            wait(V, "eo_o")
-            wait(V, "ev_o")
-            loc, lb = T.ob, me["out"][rank]
-        else:
-            wait(V, "a_ys")
-            wait(S, "a_ys")
-            if ln[1]:
-                y0 = off[rank][c2]
-                inc(S.activation(T.yb[:, y0:y0 + ln[1]], T.ys[:, ln[0]:ln[0] + ln[1]], copy), "yc")
-            loc, lb = T.ys, 0
-        wait(V, "a_" + yf)
-        for c, l, r in ((c1, lb, rn[0] + rn[1]), (c3, lb + ln[0] + ln[1], 0)):
-            n = cnt[rank][c]
+    wait(Te, "a_ws")
+    if not is_rank:
+        wait(g, "a_w1")
+        send(R, codes("vq", 0, 256), codes("vq", 0, 256), NEAR, "a_w1")
+        wait(g, "a_ws")
+        send(R, T.vs[:, 0:384], T.vs[:, 0:384], NEAR, "a_ws")
+        wait(g, "a_w2")
+        send(R, codes("vq", 256, 384), codes("vq", 256, 384), NEAR, "a_w2")
+        for j in F:
+            n, o = early_n(rank, j), me["out"][j]
+            b = me["n"][j] - n if me["early"] == 2 else 0
             if n:
-                y0 = off[rank][c]
-                inc(V.tensor_tensor(T.yb[:, y0:y0 + n], loc[:, l:l + n], T[yf][:, r:r + n], add), "yv")
-    wait(Sy, "yv")
-    wait(Sy, "yc")
-    inc(Sy.dma_start(T.y[:, :], T.yb[:]), "st", 16)
-    wait(Sy, "st")
+                wait(g, "eo_" + tag_of(j))
+                send(cores[j], T["yf%d" % me["place"]][:, b:b + n], T.ob[:, o + b:o + b + n], ALL, "a_ye%d" % me["place"])
+    front(1)
+    middle(1)
+    wait(Te, "a_w2")
+    back(1)
+    if stages[1]["m"]:
+        wait(V, "p1")
+        wait(V, "gb1")
+    for j in grp:
+        evac(1, j)
+        if j == rank or not me["n"][j]:
+            continue
+        n, o = me["n"][j], me["out"][j]
+        if is_rank:
+            wait(g, "eo_" + tag_of(j))
+            wait(g, "ev_" + tag_of(j))
+            send(cores[j], T.ys[:, 0:n], T.ob[:, o:o + n], NSIB, "a_ys")
+        else:
+            ne = early_n(rank, j)
+            a, b = (0, n - ne) if me["early"] == 2 else (ne, n)
+            wait(g, "eo_" + tag_of(j))
+            if b > a:
+                wait(g, "ev_" + tag_of(j))
+                send(cores[j], T["yf%d" % me["place"]][:, a:b], T.ob[:, o + a:o + b], ALL, "a_yf%d" % me["place"])
+
+    if is_rank:
+        for late in (False, True):
+            for q in (rank, sib):
+                fq = F[P[q]["place"]]
+                yf, sem = "yf%d" % P[q]["place"], ("a_yf%d" if late else "a_ye%d") % P[q]["place"]
+                c1, c2, c3 = P[q]["cls"]
+                ln, rn = [cnt[rank][c] for c in P[q]["cls"]], [cnt[rank][c] for c in P[fq]["cls"]]
+                if late:
+                    wait(S, sem)
+                    if rn[1]:
+                        y0 = off[rank][P[fq]["cls"][1]]
+                        inc(S.activation(T.yb[:, y0:y0 + rn[1]], T[yf][:, rn[0]:rn[0] + rn[1]], copy), "yc")
+                if q == rank:
+                    wait(V, "eo_o")
+                    wait(V, "ev_o")
+                    loc, lb = T.ob, me["out"][rank]
+                else:
+                    wait(V, "a_ys")
+                    if ln[1] and not late:
+                        wait(S, "a_ys")
+                        y0 = off[rank][c2]
+                        inc(S.activation(T.yb[:, y0:y0 + ln[1]], T.ys[:, ln[0]:ln[0] + ln[1]], copy), "yc")
+                    loc, lb = T.ys, 0
+                wait(V, sem)
+                for i, c, l, r in ((2, c1, lb, rn[0] + rn[1]), (0, c3, lb + ln[0] + ln[1], 0)):
+                    n = cnt[rank][c]
+                    if n and (P[fq]["early"] == i) != late:
+                        y0 = off[rank][c]
+                        inc(V.tensor_tensor(T.yb[:, y0:y0 + n], loc[:, l:l + n], T[yf][:, r:r + n], add), "yv")
+        wait(Sy, "yv")
+        wait(Sy, "yc")
+        inc(Sy.dma_start(T.y[:, :], T.yb[:]), "st", 16)
+        wait(Sy, "st")
     wait(g, "loc")
     for q in SEMAPHORES:
-        assert seen[q] == have[q], q
+        assert seen[q] == have[q], (core, q)

@@ -22,8 +22,9 @@ SCRATCH = {
     "yb": ("sbuf", [128, 256], "float32"), "ys": ("sbuf", [128, 256], "float32"),
     "yf0": ("sbuf", [128, 256], "float32"), "yf1": ("sbuf", [128, 256], "float32"),
 }
-SEMAPHORES = ["ld_g", "ld_go", "ld_gl", "ld_w1", "ld_w2", "ld_x", "qw1", "qw2", "qx0", "qx1", "pad", "loc", "o_w1", "o_w2", "o_ws",
-              "a_g", "a_w1", "a_w2", "a_ws", "a_f0", "a_f1", "a_s", "a_yf0", "a_yf1", "a_ye0", "a_ye1", "a_ys", "yv", "yc", "st"]
+SEMAPHORES = ["ld_g", "ld_go", "ld_gl", "ld_w10", "ld_w11", "ld_w2", "ld_x", "qw10", "qw11", "qw2", "qx0", "qx1", "pad", "loc", "o_w1",
+              "o_w2", "o_ws", "a_g", "a_w10", "a_w11", "a_w2", "a_ws", "a_f0", "a_f1", "a_s", "a_yf0", "a_yf1", "a_ye0", "a_ye1", "a_ys",
+              "a_yse", "yv", "yc", "st"]
 for _k in range(2):
     SCRATCH["h%d" % _k] = ("sbuf", [128, 2048], "bfloat16")
     SCRATCH["hq%d" % _k] = ("sbuf", [128, 512], "float8_e4m3fn_x4")
@@ -66,12 +67,12 @@ def near_engines(cores, src, dst, topo):
     return [i for i in listed(topo.mask(src, dst)) if i not in off]
 
 
-def w1_engines(far):
+def cable_engines(far):
     return far[0::2]
 
 
 def token_engines(far, i):
-    return far[1::2] if i == 0 else far[0::2]
+    return (far[0::2] if i else far[1::2]), far[1::2]
 
 
 def up16(n):
@@ -103,7 +104,7 @@ def make_plan(T, topo):
             c1, c2, c3 = P[q]["cls"]
             fq = p["f"][P[q]["place"]]
             d = P[fq]["cls"]
-            assert d[0] == c3 and d[2] == c1
+            assert d[0] == c3 and d[2] == c1 and P[q]["early"] != P[fq]["early"]
             runs = []
             for i, c in enumerate((c1, c2, c3, d[1], c1)):
                 if i == 0:
@@ -165,10 +166,11 @@ def rank_program(g, core, T, topo):
         ins.then_inc(T.sem[name], n)
         have[name] += n
 
-    def wait(queue, name):
-        if have[name]:
-            queue.wait_ge(T.sem[name], have[name])
-            seen[name] = have[name]
+    def wait(queue, *names):
+        for name in names:
+            if have[name]:
+                queue.wait_ge(T.sem[name], have[name])
+                seen[name] = have[name]
 
     def far(src):
         return far_engines(cores, src, topo)
@@ -187,35 +189,36 @@ def rank_program(g, core, T, topo):
     def codes(t, a, b):
         return T[t][:, a:b].bitcast(dt.uint8)
 
-    def early_n(r, j):
-        return cnt[j][P[r]["cls"][P[r]["early"]]]
+    def split(r, j):
+        n, ne = P[r]["n"][j], cnt[j][P[r]["cls"][P[r]["early"]]]
+        return ((n - ne, n), (0, n - ne)) if P[r]["early"] == 2 else ((0, ne), (ne, n))
 
     if is_rank:
         sources = [sib]
         if me["n"][sib]:
             have["a_g"] += len(far(cores[sib])[0::2])
             have["a_s"] += 2 * len(near(cores[sib], core))
-        if P[sib]["n"][rank]:
-            have["a_ys"] += len(near(cores[sib], core))
-        for s in ("a_w1", "a_ws", "a_w2"):
+        for (a, b), s in zip(split(sib, rank), ("a_yse", "a_ys")):
+            if b > a:
+                have[s] += len(near(cores[sib], core))
+        for s in ("a_w10", "a_w11", "a_ws", "a_w2"):
             have[s] += len(near(H, core))
         for j in F:
-            ne = early_n(j, rank)
-            if ne:
-                have["a_ye%d" % P[j]["place"]] += len(far(help_of(j)))
-            if P[j]["n"][rank] > ne:
-                have["a_yf%d" % P[j]["place"]] += len(far(help_of(j)))
+            for (a, b), s in zip(split(j, rank), ("a_ye%d", "a_yf%d")):
+                if b > a:
+                    have[s % P[j]["place"]] += len(far(help_of(j)))
     else:
         sources = F
         for j in F:
             if me["n"][j]:
                 have["a_g"] += len(far(cores[j])[0::2])
                 i = [P[q]["place"] for q in P[j]["order"]].index(me["place"])
-                have["a_f%d" % P[j]["place"]] += 2 * len(token_engines(far(cores[j]), i))
+                have["a_f%d" % P[j]["place"]] += sum(len(e) for e in token_engines(far(cores[j]), i))
         for s in ("o_w1", "o_w2", "o_ws"):
             have[s] += len(near(R, core))
-        have["a_w1"] += len(w1_engines(far(cores[pair])))
-        for s in ("a_w2", "a_ws"):
+        for s in ("a_w10", "a_w11"):
+            have[s] += len(cable_engines(far(cores[pair])))
+        for s in ("a_ws", "a_w2"):
             have[s] += len(far(help_of(pair)))
 
     grp = [sib, rank] if is_rank else F
@@ -243,10 +246,12 @@ def rank_program(g, core, T, topo):
 
     if is_rank:
         NEAR, NSIB = near(core, H), near(core, cores[sib])
-        EV = far(core)[0::2]
-        inc(Sy.dma_start(T.xb[:, 4 * NC:4 * (NC + MIN)], T.w2[:, :]), "ld_w2", 16)
+        FAR = far(core)
+        EV = FAR[0::2]
         inc(S.dma_start(T.gsrc[:], T.gt[:, :]), "ld_g", 16)
-        inc(S.dma_start(T.wb[:, 0:1024], T.w1[:, :]), "ld_w1", 16)
+        inc(Sy.dma_start(T.wb[:, 0:512], T.w1[:, 0:512]), "ld_w10", 16)
+        inc(S.dma_start(T.wb[:, 512:1024], T.w1[:, 512:1024]), "ld_w11", 16)
+        inc(Sy.dma_start(T.xb[:, 4 * NC:4 * (NC + MIN)], T.w2[:, :]), "ld_w2", 16)
         inc(Sy.dma_start(T.xb[:, 0:4 * NC], T.x[:, :]), "ld_x", 16)
         inc(Sy.dma_start(T.gr[0:1, 0:GATE_ROW], T.gt[:, :]), "ld_go", 16)
 
@@ -267,10 +272,12 @@ def rank_program(g, core, T, topo):
             inc(V.memset(T["h%d" % k][:, 4 * st["m"]:4 * MIN], 0.0), "pad")
 
     if is_rank:
+        for i in range(2):
+            wait(V, "ld_w1%d" % i)
+            a, b = MIN * i, MIN * i + MIN
+            inc(V.quantize_mx(T.wq[:, a:b], T.ws[:, a:b], T.wb[:, 4 * a:4 * b]), "qw1%d" % i)
         wait(V, "ld_w2")
         inc(V.quantize_mx(T.wq[:, 256:384], T.ws[:, 256:384], T.xb[:, 4 * NC:4 * (NC + MIN)]), "qw2")
-        wait(V, "ld_w1")
-        inc(V.quantize_mx(T.wq[:, 0:256], T.ws[:, 0:256], T.wb[:, 0:1024]), "qw1")
         wait(V, "ld_x")
         for i, q in enumerate(me["order"]):
             end = 0
@@ -283,27 +290,28 @@ def rank_program(g, core, T, topo):
         def send_x(j, d, tag, eng):
             if P[j]["n"][rank]:
                 n, a, b = P[j]["sent"][rank], me["win"][j], P[j]["land"][rank]
-                send(d, codes("xq", b, b + n), codes("xq", a, a + n), eng, tag)
-                send(d, T.xs[:, b:b + n], T.xs[:, a:a + n], eng, tag)
+                send(d, codes("xq", b, b + n), codes("xq", a, a + n), eng[0], tag)
+                send(d, T.xs[:, b:b + n], T.xs[:, a:a + n], eng[1], tag)
 
+        for i in range(2):
+            wait(g, "qw1%d" % i)
+            send(help_of(pair), codes("vq", MIN * i, MIN * i + MIN), codes("wq", MIN * i, MIN * i + MIN), cable_engines(FAR), "a_w1%d" % i)
         wait(g, "qw2")
-        send(H, codes("wq", 256, 384), codes("wq", 256, 384), NEAR, "o_w2")
-        wait(g, "qw1")
-        send(help_of(pair), codes("vq", 0, 256), codes("wq", 0, 256), w1_engines(far(core)), "a_w1")
         send(H, T.ws[:, 0:384], T.ws[:, 0:384], NEAR, "o_ws")
+        send(H, codes("wq", 256, 384), codes("wq", 256, 384), NEAR, "o_w2")
         for i, q in enumerate(me["order"]):
             wait(g, "qx%d" % i)
             j = F[P[q]["place"]]
-            send_x(j, help_of(j), "a_f%d" % me["place"], token_engines(far(core), i))
+            send_x(j, help_of(j), "a_f%d" % me["place"], token_engines(FAR, i))
             if i == 0:
                 send(H, codes("wq", 0, 256), codes("wq", 0, 256), NEAR, "o_w1")
-        send_x(sib, cores[sib], "a_s", NSIB)
+        send_x(sib, cores[sib], "a_s", (NSIB, NSIB))
     else:
         ALL, NEAR = far(core), near(core, R)
-        wait(g, "o_w2")
-        send(help_of(pair), codes("vq", 256, 384), codes("wq", 256, 384), ALL, "a_w2")
         wait(g, "o_ws")
         send(help_of(pair), T.vs[:, 0:384], T.ws[:, 0:384], ALL, "a_ws")
+        wait(g, "o_w2")
+        send(help_of(pair), codes("vq", 256, 384), codes("wq", 256, 384), ALL, "a_w2")
 
     wait(Sy, "a_g")
     rows = {rank: 0}
@@ -311,8 +319,7 @@ def rank_program(g, core, T, topo):
         rows[j] = (i + 1) * GATE_ROW
         src = T.gls if j == sib else T["glf%d" % P[j]["place"]]
         inc(Sy.dma_start(T.gr[0:1, rows[j]:rows[j] + GATE_ROW], src[:]), "ld_gl", 16)
-    wait(S, "ld_go")
-    wait(S, "ld_gl")
+    wait(S, "ld_go", "ld_gl")
     for k, st in enumerate(stages):
         for j, x0, m, n in st["runs"]:
             d = st["g0"] + m
@@ -325,14 +332,14 @@ def rank_program(g, core, T, topo):
             wait(g, "gc%d" % k)
             inc(g.partition_broadcast(T.gb[:, st["g0"]:st["g0"] + st["m"]], T.ga[0:1, st["g0"]:st["g0"] + st["m"]], 128), "gb%d" % k)
 
-    def front(k):
+    def front(k, i):
         st = stages[k]
         if not st["m"]:
             return
         q, s = ("wq", "ws") if st["own"] else ("vq", "vs")
-        for i, z in enumerate(("za%d" % k, "zb%d" % k)):
-            inc(Te.matmul_mx(T[z][:, 0:st["z1"] - st["z0"]], T[q][:, 128 * i:128 * i + 128], T[s][:, 128 * i:128 * i + 128],
-                             T.xq[:, st["z0"]:st["z1"]], T.xs[:, st["z0"]:st["z1"]], True, True), z)
+        z = "zb%d" % k if i else "za%d" % k
+        inc(Te.matmul_mx(T[z][:, 0:st["z1"] - st["z0"]], T[q][:, 128 * i:128 * i + 128], T[s][:, 128 * i:128 * i + 128],
+                         T.xq[:, st["z0"]:st["z1"]], T.xs[:, st["z0"]:st["z1"]], True, True), z)
 
     def middle(k):
         st = stages[k]
@@ -346,9 +353,7 @@ def rank_program(g, core, T, topo):
             for i, sgn in enumerate((C, -C)):
                 inc(S.activation(h[:, 4 * m + i:4 * (m + n):4], T["za%d" % k][:, c:c + n], relu, scale=sgn), "as%d" % k)
                 inc(V.tensor_scalar(h[:, 4 * m + 2 + i:4 * (m + n):4], T["zb%d" % k][:, c:c + n], sgn, 0.0, mult, mx), "av%d" % k)
-        wait(V, "pad")
-        wait(V, "as%d" % k)
-        wait(V, "av%d" % k)
+        wait(V, "pad", "as%d" % k, "av%d" % k)
         inc(V.quantize_mx(T["hq%d" % k][:, 0:st["mp"]], T["hs%d" % k][:, 0:st["mp"]], h[:, 0:4 * st["mp"]]), "q%d" % k)
 
     def back(k):
@@ -368,78 +373,60 @@ def rank_program(g, core, T, topo):
         for jj, x0, m, n in st["runs"]:
             if jj != j:
                 continue
-            za, tag = T["za%d" % k], tag_of(j)
-            ng = [cnt[j][c] for c in me["cls"]]
-            o = me["out"][j]
-            o2 = o + ng[0]
-            g0 = st["g0"] + m
-            if st["own"]:
-                b = o + (ng[0] if st["lo"] else 0)
-                inc(V.tensor_tensor(T.ob[:, b:b + n], za[:, m:m + n], T.gb[:, g0:g0 + n], mult), "eo_" + tag)
-                continue
-            n2, nx = ng[1], n - ng[1]
-            m2, m1, bx = (m, m + n2, o2 + n2) if st["lo"] else (m + nx, m, o)
-            if n2:
-                inc(V.tensor_tensor(T.tm[:, o2:o2 + n2], za[:, m2:m2 + n2], T.gb[:, g0 + m2 - m:g0 + m2 - m + n2], mult), "t_" + tag)
-            if nx:
-                inc(V.tensor_tensor(T.ob[:, bx:bx + nx], za[:, m1:m1 + nx], T.gb[:, g0 + m1 - m:g0 + m1 - m + nx], mult), "ev_" + tag)
-            if n2:
-                wait(V, "t_" + tag)
-                wait(V, "eo_" + tag)
+            tag, g0 = tag_of(j), st["g0"] + m
+            n1, n2 = [cnt[j][c] for c in me["cls"][:2]]
+            o2 = me["out"][j] + n1
+            b = o2 if st["lo"] else o2 - n1
+            out = (T.ob if st["own"] else T.tm)[:, b:b + n]
+            inc(V.tensor_tensor(out, T["za%d" % k][:, m:m + n], T.gb[:, g0:g0 + n], mult),
+                "eo_" + tag if st["own"] else "t_" + tag if n2 else "ev_" + tag)
+            if n2 and not st["own"]:
+                wait(V, "t_" + tag, "eo_" + tag)
                 y0 = off[rank][me["cls"][1]]
-                out = T.yb[:, y0:y0 + n2] if j == rank else T.ob[:, o2:o2 + n2]
-                inc(V.tensor_tensor(out, T.ob[:, o2:o2 + n2], T.tm[:, o2:o2 + n2], add), "yv" if j == rank else "ev_" + tag)
+                out = T.yb[:, y0:y0 + n2] if j == rank else T.tm[:, o2:o2 + n2]
+                inc(V.tensor_tensor(out, T.tm[:, o2:o2 + n2], T.ob[:, o2:o2 + n2], add), "yv" if j == rank else "ev_" + tag)
 
-    for s in ("qw1", "qw2", "qx0", "qx1", "a_s") if is_rank else ("o_w1", "o_ws", "a_f0", "a_f1"):
-        wait(Te, s)
-    front(0)
+    def give(j, late):
+        (a, b), o, tag = split(rank, j)[late], me["out"][j], tag_of(j)
+        if b == a:
+            return
+        wait(g, ("ev_" if late else "eo_") + tag)
+        d, eng = ("ys", NSIB) if is_rank else ("yf%d" % me["place"], ALL)
+        s = ("a_ys" if late else "a_yse") if is_rank else ("a_yf%d" if late else "a_ye%d") % me["place"]
+        send(cores[j], T[d][:, a:b], (T.tm if late else T.ob)[:, o + a:o + b], eng, s)
+
+    wait(Te, *(("qw10", "qw11", "qw2", "qx0", "qx1", "a_s") if is_rank else ("o_w1", "o_ws", "a_f0", "a_f1")))
+    front(0, 0)
+    front(0, 1)
     middle(0)
     wait(Te, "o_w2")
     back(0)
     if stages[0]["m"]:
-        wait(V, "p0")
-        wait(V, "gb0")
+        wait(V, "p0", "gb0")
     for j in grp:
         evac(0, j)
 
-    wait(Te, "a_w1")
-    wait(Te, "a_ws")
     if not is_rank:
-        wait(g, "a_w1")
-        send(R, codes("vq", 0, 256), codes("vq", 0, 256), NEAR, "a_w1")
-        wait(g, "a_ws")
-        send(R, T.vs[:, 0:384], T.vs[:, 0:384], NEAR, "a_ws")
-        wait(g, "a_w2")
-        send(R, codes("vq", 256, 384), codes("vq", 256, 384), NEAR, "a_w2")
-        for j in F:
-            n, o = early_n(rank, j), me["out"][j]
-            b = me["n"][j] - n if me["early"] == 2 else 0
-            if n:
-                wait(g, "eo_" + tag_of(j))
-                send(cores[j], T["yf%d" % me["place"]][:, b:b + n], T.ob[:, o + b:o + b + n], ALL, "a_ye%d" % me["place"])
-    front(1)
+        for s, b, lo, hi in (("a_w10", "vq", 0, 128), ("a_ws", "vs", 0, 384), ("a_w11", "vq", 128, 256), ("a_w2", "vq", 256, 384)):
+            wait(g, s)
+            piece = T.vs[:, lo:hi] if b == "vs" else codes(b, lo, hi)
+            send(R, piece, piece, NEAR, s)
+    for j in grp:
+        if j != rank:
+            give(j, False)
+    wait(Te, "a_w10", "a_ws")
+    front(1, 0)
+    wait(Te, "a_w11")
+    front(1, 1)
     middle(1)
     wait(Te, "a_w2")
     back(1)
     if stages[1]["m"]:
-        wait(V, "p1")
-        wait(V, "gb1")
+        wait(V, "p1", "gb1")
     for j in grp:
         evac(1, j)
-        if j == rank or not me["n"][j]:
-            continue
-        n, o = me["n"][j], me["out"][j]
-        if is_rank:
-            wait(g, "eo_" + tag_of(j))
-            wait(g, "ev_" + tag_of(j))
-            send(cores[j], T.ys[:, 0:n], T.ob[:, o:o + n], NSIB, "a_ys")
-        else:
-            ne = early_n(rank, j)
-            a, b = (0, n - ne) if me["early"] == 2 else (ne, n)
-            wait(g, "eo_" + tag_of(j))
-            if b > a:
-                wait(g, "ev_" + tag_of(j))
-                send(cores[j], T["yf%d" % me["place"]][:, a:b], T.ob[:, o + a:o + b], ALL, "a_yf%d" % me["place"])
+        if j != rank:
+            give(j, True)
 
     if is_rank:
         for late in (False, True):
@@ -448,32 +435,30 @@ def rank_program(g, core, T, topo):
                 yf, sem = "yf%d" % P[q]["place"], ("a_yf%d" if late else "a_ye%d") % P[q]["place"]
                 c1, c2, c3 = P[q]["cls"]
                 ln, rn = [cnt[rank][c] for c in P[q]["cls"]], [cnt[rank][c] for c in P[fq]["cls"]]
-                if late:
-                    wait(S, sem)
-                    if rn[1]:
-                        y0 = off[rank][P[fq]["cls"][1]]
-                        inc(S.activation(T.yb[:, y0:y0 + rn[1]], T[yf][:, rn[0]:rn[0] + rn[1]], copy), "yc")
                 if q == rank:
-                    wait(V, "eo_o")
-                    wait(V, "ev_o")
-                    loc, lb = T.ob, me["out"][rank]
+                    loc, lb, arr = (T.tm if late else T.ob), me["out"][rank], (("t_o", "ev_o") if late else ("eo_o",))
                 else:
-                    wait(V, "a_ys")
-                    if ln[1] and not late:
-                        wait(S, "a_ys")
-                        y0 = off[rank][c2]
-                        inc(S.activation(T.yb[:, y0:y0 + ln[1]], T.ys[:, ln[0]:ln[0] + ln[1]], copy), "yc")
-                    loc, lb = T.ys, 0
+                    loc, lb, arr = T.ys, 0, ("a_ys" if late else "a_yse",)
+                wait(V, *arr)
                 wait(V, sem)
                 for i, c, l, r in ((2, c1, lb, rn[0] + rn[1]), (0, c3, lb + ln[0] + ln[1], 0)):
                     n = cnt[rank][c]
                     if n and (P[fq]["early"] == i) != late:
                         y0 = off[rank][c]
                         inc(V.tensor_tensor(T.yb[:, y0:y0 + n], loc[:, l:l + n], T[yf][:, r:r + n], add), "yv")
-        wait(Sy, "yv")
-        wait(Sy, "yc")
+                if late and q == sib:
+                    wait(S, "a_ys")
+                    if ln[1]:
+                        y0 = off[rank][c2]
+                        inc(S.activation(T.yb[:, y0:y0 + ln[1]], T.ys[:, ln[0]:ln[0] + ln[1]], copy), "yc")
+                if late:
+                    wait(S, sem)
+                    if rn[1]:
+                        y0 = off[rank][P[fq]["cls"][1]]
+                        inc(S.activation(T.yb[:, y0:y0 + rn[1]], T[yf][:, rn[0]:rn[0] + rn[1]], copy), "yc")
+        wait(Sy, "yv", "yc")
         inc(Sy.dma_start(T.y[:, :], T.yb[:]), "st", 16)
         wait(Sy, "st")
     wait(g, "loc")
     for q in SEMAPHORES:
-        assert seen[q] == have[q], (core, q)
+        assert seen[q] == have[q], (core, q, seen[q], have[q])

import numpy as np
from concourse.bass import DstId, RemoteDMATransfer
from concourse.mybir import dt, AluOpType, ActivationFunctionType

N, NC, S2 = 8, 256, 2
WORLD = 512
C = float(np.float32(0.023))
MIN = 128
GATE_ROW = 2 * NC
WIN_MIN = 16

SCRATCH = {
    "gsrc": ("dram", [128, 4], "bfloat16"), "gls": ("dram", [128, 4], "bfloat16"),
    "glf0": ("dram", [128, 4], "bfloat16"), "glf1": ("dram", [128, 4], "bfloat16"),
    "gr": ("sbuf", [128, 4 * GATE_ROW], "bfloat16"), "ga": ("sbuf", [128, 1024], "bfloat16"), "gb": ("sbuf", [128, 1024], "bfloat16"),
    "wb": ("sbuf", [128, 1024], "bfloat16"),
    "wq": ("sbuf", [128, 384], "float8_e4m3fn_x4"), "ws": ("sbuf", [128, 384], "uint8"),
    "vq": ("sbuf", [128, 384], "float8_e4m3fn_x4"), "vs": ("sbuf", [128, 384], "uint8"),
    "xb": ("sbuf", [128, 4 * (NC + MIN)], "bfloat16"),
    "xq": ("sbuf", [128, 1536], "float8_e4m3fn_x4"), "xs": ("sbuf", [128, 1536], "uint8"),
    "ob": ("sbuf", [128, 1024], "float32"), "tm": ("sbuf", [128, 1024], "float32"),
    "yb": ("sbuf", [128, 256], "float32"), "ys": ("sbuf", [128, 256], "float32"),
    "yf0": ("sbuf", [128, 256], "float32"), "yf1": ("sbuf", [128, 256], "float32"),
}
SEMAPHORES = ["ld_g", "ld_go", "ld_gl", "ld_w10", "ld_w11", "ld_w2", "ld_x", "qw10", "qw11", "qw2", "qx0", "qx1", "pad", "loc", "o_w1",
              "o_w2", "o_ws", "a_g", "a_w10", "a_w11", "a_w2", "a_ws", "a_f0", "a_f1", "a_s", "a_yf0", "a_yf1", "a_ye0", "a_ye1", "a_ys",
              "a_yse", "yv", "yc", "st"]
for _k in range(2):
    SCRATCH["h%d" % _k] = ("sbuf", [128, 2048], "bfloat16")
    SCRATCH["hq%d" % _k] = ("sbuf", [128, 512], "float8_e4m3fn_x4")
    SCRATCH["hs%d" % _k] = ("sbuf", [128, 512], "uint8")
    SCRATCH["za%d" % _k] = ("psum", [128, 512], "float32")
    SCRATCH["zb%d" % _k] = ("psum", [128, 512], "float32")
    SEMAPHORES += ["%s%d" % (s, _k) for s in ("za", "zb", "as", "av", "q", "p", "gc", "gb")]
for _s in ("f0", "f1", "s", "o"):
    SEMAPHORES += ["eo_" + _s, "ev_" + _s, "t_" + _s]
_HELP = {}


def helper(c, topo):
    if c not in _HELP:
        def port(k):
            return any(topo.mates(k, d) and topo.may_write(k, d) for d in range(WORLD))
        _HELP[c] = [k for k in range(WORLD) if topo.host(k) == topo.host(c) and topo.chip(k) == topo.chip(c)
                    and topo.die(k) != topo.die(c) and port(k) == port(c)][0]
    return _HELP[c]


def bits(lst):
    return sum(1 << i for i in lst)


def listed(mask):
    return [i for i in range(16) if mask >> i & 1]


def far_engines(cores, src, topo):
    m = -1
    for d in cores:
        if d != src and topo.may_write(src, d):
            m &= topo.mask(src, d)
    return listed(m)


def near_engines(cores, src, dst, topo):
    off = far_engines(cores, src, topo)
    return [i for i in listed(topo.mask(src, dst)) if i not in off]


def cable_engines(far):
    return far[0::2]


def token_engines(far, i):
    return (far[0::2] if i else far[1::2]), far[1::2]


def up16(n):
    return -(-n // WIN_MIN) * WIN_MIN


def make_plan(T, topo):
    cores, cnt = T.cores, T.tables["CNT"]
    off = [[sum(c[:e]) for e in range(N + 1)] for c in cnt]
    host = [topo.host(c) for c in cores]
    P = []
    for r in range(N):
        home = [j for j in range(N) if host[j] == host[r]]
        sib = [j for j in home if j != r][0]
        place = home.index(r)
        rack = topo.rack(host[r])
        far = [j for j in range(N) if topo.rack(host[j]) != rack and topo.may_write(cores[r], cores[j])]
        other = [j for j in range(N) if topo.rack(host[j]) == rack and host[j] != host[r]]
        pair = far[place]
        a, b = (r, pair) if (r + S2) % N == pair else (pair, r)
        P.append({"sib": sib, "place": place, "pair": pair, "f": other, "a": a, "b": b, "cls": [(a - S2) % N, a, b],
                  "early": 0 if r == a else 2})
    for r in range(N):
        p = P[r]
        p["n"] = {j: sum(cnt[j][c] for c in p["cls"]) for j in [r, p["sib"]] + p["f"]}
        own0 = up16(p["n"][p["sib"]])
        at, win, p["chain"] = own0, {}, {}
        for q in (r, p["sib"]):
            c1, c2, c3 = P[q]["cls"]
            fq = p["f"][P[q]["place"]]
            d = P[fq]["cls"]
            assert d[0] == c3 and d[2] == c1 and P[q]["early"] != P[fq]["early"]
            runs = []
            for i, c in enumerate((c1, c2, c3, d[1], c1)):
                if i == 0:
                    win[q] = at
                if i == 2:
                    win[fq] = at
                if cnt[r][c]:
                    if runs and runs[-1][1] + runs[-1][2] == off[r][c]:
                        runs[-1][2] += cnt[r][c]
                    else:
                        runs.append([at, off[r][c], cnt[r][c]])
                at += cnt[r][c]
            runs = [[o, s, max(n, MIN)] for o, s, n in runs]
            at = up16(runs[-1][0] + runs[-1][2])
            runs[-1][2] = at - runs[-1][0]
            p["chain"][q] = runs
            assert max(s + n for o, s, n in runs) <= NC + MIN
        p["win"], p["end"] = win, at
        p["land"] = {p["sib"]: own0 - p["n"][p["sib"]], r: own0,
                     p["f"][0]: 0, p["f"][1]: p["n"][p["f"][0]]}
        p["out"] = {}
        for grp in (p["f"], [p["sib"], r]):
            o = 0
            for j in grp:
                p["out"][j] = o
                o += p["n"][j]
    for r in range(N):
        p = P[r]
        p["sent"] = dict(p["n"])
        j = p["f"][1]
        if p["n"][j]:
            p["sent"][j] = max(p["n"][j], MIN - p["n"][p["f"][0]])
        assert sum(p["sent"][j] for j in p["f"]) >= MIN and P[j]["win"][r] + p["sent"][j] <= P[j]["end"]
        big = max(p["f"], key=lambda j: P[j]["n"][r])
        p["order"] = sorted((r, p["sib"]), key=lambda q: P[q]["place"] != P[big]["place"])
    return P, cnt, off


def rank_program(g, core, T, topo):
    cores = T.cores
    rank = T.rank_of(core)
    is_rank = rank is not None
    if not is_rank:
        mine = [r for r in range(N) if helper(cores[r], topo) == core]
        if not mine:
            return
        rank = mine[0]
    P, cnt, off = make_plan(T, topo)
    me = P[rank]
    R, H = cores[rank], helper(cores[rank], topo)
    sib, F, pair = me["sib"], me["f"], me["pair"]
    add, mult, mx = AluOpType.add, AluOpType.mult, AluOpType.max
    relu, copy = ActivationFunctionType.Relu, ActivationFunctionType.Copy
    V, S, Te, Sy = g.vector, g.scalar, g.tensor, g.sync
    have = {s: 0 for s in SEMAPHORES}
    seen = {s: 0 for s in SEMAPHORES}

    def inc(ins, name, n=1):
        ins.then_inc(T.sem[name], n)
        have[name] += n

    def wait(queue, *names):
        for name in names:
            if have[name]:
                queue.wait_ge(T.sem[name], have[name])
                seen[name] = have[name]

    def far(src):
        return far_engines(cores, src, topo)

    def near(src, dst):
        return near_engines(cores, src, dst, topo)

    def help_of(j):
        return helper(cores[j], topo)

    def send(d, out, in_, eng, sem):
        rid, pid = topo.addr(d, core)
        g.remote_dma(out, in_, T.sem[sem], T.sem.loc, pid, rid, bits(eng))
        have["loc"] += len(eng)

    def codes(t, a, b):
        return T[t][:, a:b].bitcast(dt.uint8)

    def split(r, j):
        n, ne = P[r]["n"][j], cnt[j][P[r]["cls"][P[r]["early"]]]
        return ((n - ne, n), (0, n - ne)) if P[r]["early"] == 2 else ((0, ne), (ne, n))

    if is_rank:
        sources = [sib]
        if me["n"][sib]:
            have["a_g"] += len(far(cores[sib])[0::2])
            have["a_s"] += 2 * len(near(cores[sib], core))
        for (a, b), s in zip(split(sib, rank), ("a_yse", "a_ys")):
            if b > a:
                have[s] += len(near(cores[sib], core))
        for s in ("a_w10", "a_w11", "a_ws", "a_w2"):
            have[s] += len(near(H, core))
        for j in F:
            for (a, b), s in zip(split(j, rank), ("a_ye%d", "a_yf%d")):
                if b > a:
                    have[s % P[j]["place"]] += len(far(help_of(j)))
    else:
        sources = F
        for j in F:
            if me["n"][j]:
                have["a_g"] += len(far(cores[j])[0::2])
                i = [P[q]["place"] for q in P[j]["order"]].index(me["place"])
                have["a_f%d" % P[j]["place"]] += sum(len(e) for e in token_engines(far(cores[j]), i))
        for s in ("o_w1", "o_w2", "o_ws"):
            have[s] += len(near(R, core))
        for s in ("a_w10", "a_w11"):
            have[s] += len(cable_engines(far(cores[pair])))
        for s in ("a_ws", "a_w2"):
            have[s] += len(far(help_of(pair)))

    grp = [sib, rank] if is_rank else F
    stages, at = [], 0
    for first in (True, False):
        e = rank if first else pair
        lo = 0 if e == me["a"] else 1
        cl = me["cls"][lo:lo + 2]
        runs, m = [], 0
        for j in grp:
            n = sum(cnt[j][c] for c in cl)
            if n:
                x0 = me["land"][j] + (cnt[j][me["cls"][0]] if lo else 0)
                runs.append((j, x0, m, n))
                m += n
        z0 = min([x for _, x, _, _ in runs] or [0])
        z1 = max([x + n for _, x, _, n in runs] or [0])
        if z1 - z0 < MIN:
            if not is_rank:
                z0 = max(0, z1 - MIN)
            z1 = z0 + MIN
        assert z1 - z0 <= 512
        stages.append({"lo": lo, "cl": cl, "runs": runs, "m": m, "mp": max(m, MIN), "z0": z0, "z1": z1, "own": first, "g0": at})
        at += m

    if is_rank:
        NEAR, NSIB = near(core, H), near(core, cores[sib])
        FAR = far(core)
        EV = FAR[0::2]
        inc(S.dma_start(T.gsrc[:], T.gt[:, :]), "ld_g", 16)
        inc(Sy.dma_start(T.wb[:, 0:512], T.w1[:, 0:512]), "ld_w10", 16)
        inc(S.dma_start(T.wb[:, 512:1024], T.w1[:, 512:1024]), "ld_w11", 16)
        inc(Sy.dma_start(T.xb[:, 4 * NC:4 * (NC + MIN)], T.w2[:, :]), "ld_w2", 16)
        inc(Sy.dma_start(T.xb[:, 0:4 * NC], T.x[:, :]), "ld_x", 16)
        inc(Sy.dma_start(T.gr[0:1, 0:GATE_ROW], T.gt[:, :]), "ld_go", 16)

        to = [j for j in F + [sib] if P[j]["n"][rank]]
        wait(g, "ld_g")
        if to:
            ids, dsts = [], []
            for j in to:
                rid, pid = topo.addr(cores[j] if j == sib else help_of(j), core)
                ids.append(DstId(rid=rid, pnc=pid))
                dsts.append(T["gls"][:] if j == sib else T["glf%d" % me["place"]][:])
            g.remote_dma_fused([RemoteDMATransfer(dst_ids=ids, dma_engine_mask=bits(EV), remote_sem=T.sem.a_g, srcs=[T.gsrc[:]], dsts=dsts)],
                               local_sem=T.sem.loc)
            have["loc"] += len(EV)

    for k, st in enumerate(stages):
        if st["m"] and st["m"] < MIN:
            inc(V.memset(T["h%d" % k][:, 4 * st["m"]:4 * MIN], 0.0), "pad")

    if is_rank:
        for i in range(2):
            wait(V, "ld_w1%d" % i)
            a, b = MIN * i, MIN * i + MIN
            inc(V.quantize_mx(T.wq[:, a:b], T.ws[:, a:b], T.wb[:, 4 * a:4 * b]), "qw1%d" % i)
        wait(V, "ld_w2")
        inc(V.quantize_mx(T.wq[:, 256:384], T.ws[:, 256:384], T.xb[:, 4 * NC:4 * (NC + MIN)]), "qw2")
        wait(V, "ld_x")
        for i, q in enumerate(me["order"]):
            end = 0
            for o, s, n in me["chain"][q]:
                if o < end:
                    wait(V, "qx%d" % i)
                end = o + n
                inc(V.quantize_mx(T.xq[:, o:o + n], T.xs[:, o:o + n], T.xb[:, 4 * s:4 * (s + n)]), "qx%d" % i)

        def send_x(j, d, tag, eng):
            if P[j]["n"][rank]:
                n, a, b = P[j]["sent"][rank], me["win"][j], P[j]["land"][rank]
                send(d, codes("xq", b, b + n), codes("xq", a, a + n), eng[0], tag)
                send(d, T.xs[:, b:b + n], T.xs[:, a:a + n], eng[1], tag)

        for i in range(2):
            wait(g, "qw1%d" % i)
            send(help_of(pair), codes("vq", MIN * i, MIN * i + MIN), codes("wq", MIN * i, MIN * i + MIN), cable_engines(FAR), "a_w1%d" % i)
        wait(g, "qw2")
        send(H, T.ws[:, 0:384], T.ws[:, 0:384], NEAR, "o_ws")
        send(H, codes("wq", 256, 384), codes("wq", 256, 384), NEAR, "o_w2")
        for i, q in enumerate(me["order"]):
            wait(g, "qx%d" % i)
            j = F[P[q]["place"]]
            send_x(j, help_of(j), "a_f%d" % me["place"], token_engines(FAR, i))
            if i == 0:
                send(H, codes("wq", 0, 256), codes("wq", 0, 256), NEAR, "o_w1")
        send_x(sib, cores[sib], "a_s", (NSIB, NSIB))
    else:
        ALL, NEAR = far(core), near(core, R)
        wait(g, "o_ws")
        send(help_of(pair), T.vs[:, 0:384], T.ws[:, 0:384], ALL, "a_ws")
        wait(g, "o_w2")
        send(help_of(pair), codes("vq", 256, 384), codes("wq", 256, 384), ALL, "a_w2")

    wait(Sy, "a_g")
    rows = {rank: 0}
    for i, j in enumerate([j for j in sources if me["n"][j]]):
        rows[j] = (i + 1) * GATE_ROW
        src = T.gls if j == sib else T["glf%d" % P[j]["place"]]
        inc(Sy.dma_start(T.gr[0:1, rows[j]:rows[j] + GATE_ROW], src[:]), "ld_gl", 16)
    wait(S, "ld_go", "ld_gl")
    for k, st in enumerate(stages):
        for j, x0, m, n in st["runs"]:
            d = st["g0"] + m
            for c, row in ((st["cl"][0], 1), (st["cl"][1], 0)):
                if cnt[j][c]:
                    s = rows[j] + row * NC + off[j][c]
                    inc(S.activation(T.ga[0:1, d:d + cnt[j][c]], T.gr[0:1, s:s + cnt[j][c]], copy), "gc%d" % k)
                    d += cnt[j][c]
        if st["m"]:
            wait(g, "gc%d" % k)
            inc(g.partition_broadcast(T.gb[:, st["g0"]:st["g0"] + st["m"]], T.ga[0:1, st["g0"]:st["g0"] + st["m"]], 128), "gb%d" % k)

    def front(k, i):
        st = stages[k]
        if not st["m"]:
            return
        q, s = ("wq", "ws") if st["own"] else ("vq", "vs")
        z = "zb%d" % k if i else "za%d" % k
        inc(Te.matmul_mx(T[z][:, 0:st["z1"] - st["z0"]], T[q][:, 128 * i:128 * i + 128], T[s][:, 128 * i:128 * i + 128],
                         T.xq[:, st["z0"]:st["z1"]], T.xs[:, st["z0"]:st["z1"]], True, True), z)

    def middle(k):
        st = stages[k]
        if not st["m"]:
            return
        h = T["h%d" % k]
        wait(S, "za%d" % k)
        wait(V, "zb%d" % k)
        for j, x0, m, n in st["runs"]:
            c = x0 - st["z0"]
            for i, sgn in enumerate((C, -C)):
                inc(S.activation(h[:, 4 * m + i:4 * (m + n):4], T["za%d" % k][:, c:c + n], relu, scale=sgn), "as%d" % k)
                inc(V.tensor_scalar(h[:, 4 * m + 2 + i:4 * (m + n):4], T["zb%d" % k][:, c:c + n], sgn, 0.0, mult, mx), "av%d" % k)
        wait(V, "pad", "as%d" % k, "av%d" % k)
        inc(V.quantize_mx(T["hq%d" % k][:, 0:st["mp"]], T["hs%d" % k][:, 0:st["mp"]], h[:, 0:4 * st["mp"]]), "q%d" % k)

    def back(k):
        st = stages[k]
        if not st["m"]:
            return
        q, s = ("wq", "ws") if st["own"] else ("vq", "vs")
        wait(Te, "q%d" % k)
        inc(Te.matmul_mx(T["za%d" % k][:, 0:st["mp"]], T[q][:, 256:384], T[s][:, 256:384],
                         T["hq%d" % k][:, 0:st["mp"]], T["hs%d" % k][:, 0:st["mp"]], True, True), "p%d" % k)

    def tag_of(j):
        return "o" if j == rank else "s" if j == sib else "f%d" % P[j]["place"]

    def evac(k, j):
        st = stages[k]
        for jj, x0, m, n in st["runs"]:
            if jj != j:
                continue
            tag, g0 = tag_of(j), st["g0"] + m
            n1, n2 = [cnt[j][c] for c in me["cls"][:2]]
            o2 = me["out"][j] + n1
            b = o2 if st["lo"] else o2 - n1
            out = (T.ob if st["own"] else T.tm)[:, b:b + n]
            inc(V.tensor_tensor(out, T["za%d" % k][:, m:m + n], T.gb[:, g0:g0 + n], mult),
                "eo_" + tag if st["own"] else "t_" + tag if n2 else "ev_" + tag)
            if n2 and not st["own"]:
                wait(V, "t_" + tag, "eo_" + tag)
                y0 = off[rank][me["cls"][1]]
                out = T.yb[:, y0:y0 + n2] if j == rank else T.tm[:, o2:o2 + n2]
                inc(V.tensor_tensor(out, T.tm[:, o2:o2 + n2], T.ob[:, o2:o2 + n2], add), "yv" if j == rank else "ev_" + tag)

    def give(j, late):
        (a, b), o, tag = split(rank, j)[late], me["out"][j], tag_of(j)
        if b == a:
            return
        wait(g, ("ev_" if late else "eo_") + tag)
        d, eng = ("ys", NSIB) if is_rank else ("yf%d" % me["place"], ALL)
        s = ("a_ys" if late else "a_yse") if is_rank else ("a_yf%d" if late else "a_ye%d") % me["place"]
        send(cores[j], T[d][:, a:b], (T.tm if late else T.ob)[:, o + a:o + b], eng, s)

    wait(Te, *(("qw10", "qw11", "qw2", "qx0", "qx1", "a_s") if is_rank else ("o_w1", "o_ws", "a_f0", "a_f1")))
    front(0, 0)
    front(0, 1)
    middle(0)
    wait(Te, "o_w2")
    back(0)
    if stages[0]["m"]:
        wait(V, "p0", "gb0")
    for j in grp:
        evac(0, j)

    if not is_rank:
        for s, b, lo, hi in (("a_w10", "vq", 0, 128), ("a_ws", "vs", 0, 384), ("a_w11", "vq", 128, 256), ("a_w2", "vq", 256, 384)):
            wait(g, s)
            piece = T.vs[:, lo:hi] if b == "vs" else codes(b, lo, hi)
            send(R, piece, piece, NEAR, s)
    for j in grp:
        if j != rank:
            give(j, False)
    wait(Te, "a_w10", "a_ws")
    front(1, 0)
    wait(Te, "a_w11")
    front(1, 1)
    middle(1)
    wait(Te, "a_w2")
    back(1)
    if stages[1]["m"]:
        wait(V, "p1", "gb1")
    for j in grp:
        evac(1, j)
        if j != rank:
            give(j, True)

    if is_rank:
        for late in (False, True):
            for q in (rank, sib):
                fq = F[P[q]["place"]]
                yf, sem = "yf%d" % P[q]["place"], ("a_yf%d" if late else "a_ye%d") % P[q]["place"]
                c1, c2, c3 = P[q]["cls"]
                ln, rn = [cnt[rank][c] for c in P[q]["cls"]], [cnt[rank][c] for c in P[fq]["cls"]]
                if q == rank:
                    loc, lb, arr = (T.tm if late else T.ob), me["out"][rank], (("t_o", "ev_o") if late else ("eo_o",))
                else:
                    loc, lb, arr = T.ys, 0, ("a_ys" if late else "a_yse",)
                wait(V, *arr)
                wait(V, sem)
                for i, c, l, r in ((2, c1, lb, rn[0] + rn[1]), (0, c3, lb + ln[0] + ln[1], 0)):
                    n = cnt[rank][c]
                    if n and (P[fq]["early"] == i) != late:
                        y0 = off[rank][c]
                        inc(V.tensor_tensor(T.yb[:, y0:y0 + n], loc[:, l:l + n], T[yf][:, r:r + n], add), "yv")
                if late and q == sib:
                    wait(S, "a_ys")
                    if ln[1]:
                        y0 = off[rank][c2]
                        inc(S.activation(T.yb[:, y0:y0 + ln[1]], T.ys[:, ln[0]:ln[0] + ln[1]], copy), "yc")
                if late:
                    wait(S, sem)
                    if rn[1]:
                        y0 = off[rank][P[fq]["cls"][1]]
                        inc(S.activation(T.yb[:, y0:y0 + rn[1]], T[yf][:, rn[0]:rn[0] + rn[1]], copy), "yc")
        wait(Sy, "yv", "yc")
        inc(Sy.dma_start(T.y[:, :], T.yb[:]), "st", 16)
        wait(Sy, "st")
    wait(g, "loc")
    for q in SEMAPHORES:
        assert seen[q] == have[q], (core, q, seen[q], have[q])
